import numpy as np
import ml_dtypes


def mxq(x, axis, fmt="e4m3"):
    dtype, down = {"e4m3": (ml_dtypes.float8_e4m3fn, 7), "e5m2": (ml_dtypes.float8_e5m2, 14)}[fmt]
    v = np.moveaxis(np.asarray(x, np.float32).astype(ml_dtypes.bfloat16).astype(np.float64), axis, -1)
    blocks = v.reshape(v.shape[:-1] + (-1, 32))
    amax = np.abs(blocks).max(-1, keepdims=True)
    byte = np.maximum(np.where(amax > 0, np.frexp(amax)[1] - 1 + 127, 0) - down, 1)
    scale = np.exp2(byte - 127.0)
    codes = (blocks / scale).astype(np.float32).astype(dtype).astype(np.float64)
    return np.moveaxis((codes * scale).reshape(v.shape), -1, axis)


WIDE = False


def mx_kscale(k):
    if not WIDE:
        return np.ones(k)
    levels = np.array([10, -10, 5, -5, 0])
    if k % 512:
        return np.exp2(np.random.permutation(np.resize(levels, k // 32))).repeat(32)
    a = np.empty((k // 512, 16))
    for p in range(k // 512):
        a[p, :8] = np.random.permutation(np.resize(levels, 8))
        for g in range(8):
            far = levels[np.abs(levels - a[p, g]) >= 10]
            a[p, g + 8] = far[np.random.randint(len(far))]
    return np.exp2(a.ravel()).repeat(32)


def f64(x):
    return np.asarray(x).astype(np.float64)


def striped(idx):
    return np.tile(idx.reshape(-1, 16).T, (8, 1)).astype(np.uint16)


def unstriped(offs):
    return offs[:16].T.reshape(-1).astype(np.int64)


def striped8(idx):
    return np.concatenate([x.reshape(-1, 16).T for x in idx]).astype(np.uint16)


def runs(offs, k):
    lists = np.stack([offs[16 * r : 16 * r + 16].T.reshape(-1) for r in range(8)]).astype(np.int64)
    return lists[np.arange(k) % 512 // 64]


def pack_weight(w):
    k, n = w.shape
    w = f64(np.asarray(w, np.float32).astype(ml_dtypes.bfloat16)).reshape(k // 32, 32, n)
    amax = np.abs(w).max(1)
    byte = np.clip(np.where(amax > 0, np.frexp(amax)[1] - 1 + 127 - 7, 1), 1, 254)
    scaled = (w * np.exp2(127.0 - byte)[:, None, :]).reshape(k, n).astype(np.float32)
    words = np.ascontiguousarray(scaled.reshape(k // 512, 128, 4, n).transpose(0, 1, 3, 2)).astype(ml_dtypes.float8_e4m3fn).view(np.uint8)
    return words, np.ascontiguousarray(byte.astype(np.uint8).reshape(k // 512, 16, n))


def unpack_weight(words, scales):
    g, p, n, _ = words.shape
    vals = np.ascontiguousarray(words).view(ml_dtypes.float8_e4m3fn).astype(np.float64) * np.repeat(np.exp2(scales.astype(np.float64) - 127.0), 8, axis=1)[..., None]
    return vals.transpose(0, 1, 3, 2).reshape(g * 512, n)

def planes(y):
    n, m = y.shape
    v = y.astype(np.float32).astype(ml_dtypes.bfloat16).astype(np.float64).reshape(n // 32, 32, m)
    top = np.abs(v).max(1)
    byte = np.clip(np.where(top > 0, np.frexp(top)[1] - 1 + 127 - 7, 1), 1, 254)
    codes = (v * np.exp2(127.0 - byte)[:, None, :]).reshape(n, m).astype(np.float32).astype(ml_dtypes.float8_e4m3fn).view(np.uint8)
    words = codes.reshape(n // 512, 128, 4, m).transpose(0, 1, 3, 2)
    return np.ascontiguousarray(words), np.ascontiguousarray(byte.astype(np.uint8).reshape(n // 512, 16, m))


K, T, S, N, H, W = 512, 2048, 512, 512, 512, 256


def setup_inputs():
    n = np.random.standard_normal
    s = mx_kscale(K)[:, None]
    u = mx_kscale(H)
    packed_xT = pack_weight(n((K, T)) * s)
    packed_w1 = pack_weight(n((K, H)) / np.sqrt(K) / s)
    packed_w2 = pack_weight(n((H, N)) / np.sqrt(H) / u[:, None])
    packed_w3 = pack_weight(n((H, N)) / np.sqrt(H) / u[:, None])
    return {
        "x_words": packed_xT[0],
        "x_scales": packed_xT[1],
        "w1_words": packed_w1[0],
        "w1_scales": packed_w1[1],
        "gn": (np.random.uniform(0.5, 1.5, (H, 1)) * u[:, None]).astype(np.float32),
        "w2_words": packed_w2[0],
        "w2_scales": packed_w2[1],
        "gm": (np.random.uniform(0.5, 1.5, (H, 1)) * u[:, None]).astype(np.float32),
        "w3_words": packed_w3[0],
        "w3_scales": packed_w3[1],
        "offs": striped(np.random.permutation(T)[:S]),
        "n1": striped8(np.stack([np.random.permutation(S) for _ in range(8)])),
        "n2": striped8(np.stack([np.random.permutation(S) for _ in range(8)])),
        "n3": striped8(np.stack([np.random.permutation(S) for _ in range(8)])),
        "n4": striped8(np.stack([np.random.permutation(S)[:W] for _ in range(8)])),
        "n5": striped8(np.stack([np.random.permutation(S)[:W] for _ in range(8)])),
    }


def reference(x_words, x_scales, w1_words, w1_scales, gn, w2_words, w2_scales, gm, w3_words, w3_scales, offs, n1, n2, n3, n4, n5):
    xq = unpack_weight(x_words, x_scales)[:, unstriped(offs)]
    y = unpack_weight(w1_words, w1_scales).T @ xq
    z2 = f64(gm) * (y - (y[np.arange(H)[:, None], runs(n3, H)]))
    b = unpack_weight(w3_words, w3_scales).T @ mxq(z2, 0, "e4m3")
    z = f64(gn) * (y[np.arange(H)[:, None], runs(n1, H)] + 0.75 * (y[np.arange(H)[:, None], runs(n2, H)]))
    a = unpack_weight(w2_words, w2_scales).T @ mxq(z, 0, "e4m3")
    ra = b[np.arange(N)[:, None], runs(n5, N)] - (0.5 * (a[np.arange(N)[:, None], runs(n4, N)]))
    out = a.copy()
    out[np.arange(N)[:, None], runs(n4, N)] = ra
    return (out,) + planes(out)

@@ -1,0 +1,248 @@
+from contextlib import ExitStack
+
+import concourse.mybir as mybir
+
+K, T, S, N, H, W = 512, 2048, 512, 512, 512, 256
+FLOPS = 2 * K * H * S + 2 * 2 * H * N * S
+
+F32 = mybir.dt.float32
+BF16 = mybir.dt.bfloat16
+I32 = mybir.dt.int32
+U32 = mybir.dt.uint32
+U16 = mybir.dt.uint16
+U8 = mybir.dt.uint8
+FP8X4 = mybir.dt.float8_e4m3fn_x4
+COPY = mybir.ActivationFunctionType.Copy
+MULT = mybir.AluOpType.mult
+ADD = mybir.AluOpType.add
+
+P = 128
+PACK = 4
+HALF = S // 2
+X_EARLY = 768
+
+
+def load_scales(nc, plane, scales, first):
+    for q in range(4):
+        nc.sync.dma_start(out=plane[32 * q + first : 32 * q + first + 4, :].bitcast(I32), in_=scales[0, 4 * q : 4 * q + 4, :].bitcast(I32))
+
+
+def load_words(nc, tile, words):
+    nc.sync.dma_start(out=tile[:], in_=words[0].rearrange("p n t -> p (n t)").bitcast(I32))
+
+
+def deal(nc, dealt, raw):
+    nc.vector.tensor_copy(out=dealt[:].rearrange("p (t m) -> p t m", t=PACK), in_=raw[:].rearrange("p (m t) -> p t m", t=PACK))
+
+
+def interleave(nc, grouped, rows):
+    nc.scalar.activation(
+        out=grouped[:].rearrange("p (c i t) -> p c t i", i=4, t=PACK),
+        in_=rows[:].rearrange("p t (c i) -> p c t i", i=4),
+        func=COPY,
+    )
+
+
+def tile_picked_forkputbsumdif_none_po_kernel(
+    tc, x_words, x_scales, w1_words, w1_scales, gn, w2_words, w2_scales, gm, w3_words, w3_scales, offs, n1, n2, n3, n4, n5, out_0, out_1, out_2
+):
+    nc = tc.nc
+    with ExitStack() as ctx:
+        keep = ctx.enter_context(tc.tile_pool(name="keep", bufs=1))
+        psum = ctx.enter_context(tc.psum_pool(name="psum", bufs=1))
+
+        def sb(name, shape, dtype, tag=None):
+            return keep.tile(shape, dtype, name=name, tag=tag or name, align_bytes=64)
+
+        offs_t = sb("offs_t", [P, S // 16], U16)
+        n1_t = sb("n1_t", [P, S // 16], U16)
+        n2_t = sb("n2_t", [P, S // 16], U16)
+        n3_t = sb("n3_t", [P, S // 16], U16)
+        n4_t = sb("n4_t", [P, W // 16], U16)
+        n5_t = sb("n5_t", [P, W // 16], U16)
+
+        xs_raw = sb("xs_raw", [P, T], U8)
+        xw_raw = sb("xw_raw", [P, T], I32)
+        w1s_raw = sb("w1s_raw", [P, H], U8)
+        w23s_raw = sb("w23s_raw", [P, N], U8)
+        w1w_raw = sb("w1w_raw", [P, H], I32)
+        w2w_raw = sb("w2w_raw", [P, N], I32)
+        w3w_raw = sb("w3w_raw", [P, N], I32)
+        gn_t = sb("gn_t", [P, PACK], F32)
+        gm_t = sb("gm_t", [P, PACK], F32)
+        gm_neg = sb("gm_neg", [P, PACK], F32)
+        yn = [sb("yn%d" % t, [P, 2 * S], F32) for t in range(PACK)]
+        ym = [sb("ym%d" % t, [P, 2 * S], F32) for t in range(PACK)]
+
+        nc.vector.memset(xs_raw[:].bitcast(I32), 0)
+        nc.vector.memset(w1s_raw[:].bitcast(I32), 0)
+        nc.vector.memset(yn[0][:, S:], 0.0)
+        nc.vector.memset(w23s_raw[:].bitcast(I32), 0)
+        for t in range(1, PACK):
+            nc.scalar.activation(out=yn[t][:, S:], in_=yn[0][:, S:], func=COPY)
+
+        x_flat = x_words[0].rearrange("p n t -> p (n t)").bitcast(I32)
+        nc.sync.dma_start(offs_t[:], offs)
+        nc.sync.dma_start(out=xw_raw[:, :X_EARLY], in_=x_flat[:, :X_EARLY])
+        load_scales(nc, xs_raw, x_scales, 0)
+        nc.sync.dma_start(out=xw_raw[:, X_EARLY:], in_=x_flat[:, X_EARLY:])
+        load_words(nc, w1w_raw, w1_words)
+        load_scales(nc, w1s_raw, w1_scales, 0)
+        load_words(nc, w2w_raw, w2_words)
+        load_words(nc, w3w_raw, w3_words)
+        nc.sync.dma_start(out=gn_t[:], in_=gn.rearrange("(p t) o -> p (t o)", t=PACK))
+        nc.sync.dma_start(n2_t[:], n2)
+        nc.sync.dma_start(n1_t[:], n1)
+        nc.sync.dma_start(out=gm_t[:], in_=gm.rearrange("(p t) o -> p (t o)", t=PACK))
+        nc.sync.dma_start(n3_t[:], n3)
+        load_scales(nc, w23s_raw, w2_scales, 0)
+        load_scales(nc, w23s_raw, w3_scales, 4)
+        nc.sync.dma_start(n4_t[:], n4)
+        nc.sync.dma_start(n5_t[:], n5)
+
+        xs = sb("xs", [P, S], U8)
+        xw = sb("xw", [P, S], U32)
+        w1s = sb("w1s", [P, H], U8)
+        w1w = sb("w1w", [P, H], I32)
+        w23s = sb("w23s", [P, N], U8)
+        w2w = sb("w2w", [P, N], I32)
+        w3w = sb("w3w", [P, N], I32)
+
+        nc.vector.tensor_copy(xs[:], xs_raw[:].indirect(offs_t[:]))
+        nc.vector.tensor_copy(xw[:], xw_raw[:].bitcast(U32).indirect(offs_t[:]))
+        w1w_by_t = w1w_raw[:].rearrange("p (m t) -> p t m", t=PACK)
+        w1s_by_t = w1s_raw[:].rearrange("p (m t) -> p t m", t=PACK)
+        nc.vector.tensor_copy(out=w1w[:, :P], in_=w1w_by_t[:, 0, :])
+        nc.vector.tensor_copy(out=w1s[:, :P], in_=w1s_by_t[:, 0, :])
+        nc.vector.tensor_copy(out=w1s[:, P:].rearrange("p (t m) -> p t m", m=P), in_=w1s_by_t[:, 1:, :])
+        nc.vector.tensor_copy(out=w1w[:, P:].rearrange("p (t m) -> p t m", m=P), in_=w1w_by_t[:, 1:, :])
+
+        y_ps = [psum.tile([P, S], F32, name="yb%d" % t) for t in range(PACK)]
+        for t in range(PACK):
+            cols = slice(P * t, P * (t + 1))
+            nc.tensor.matmul_mx(
+                out=y_ps[t][:], lhsT=w1w[:, cols].bitcast(FP8X4), lhsT_scale=w1s[:, cols], rhs=xw[:].bitcast(FP8X4), rhs_scale=xs[:], start=True, stop=True
+            )
+        for t in range(PACK):
+            nc.scalar.activation(out=yn[t][:, :S], in_=y_ps[t][:], func=COPY, scale=gn_t[:, t : t + 1])
+
+        deal(nc, w2w, w2w_raw)
+        deal(nc, w3w, w3w_raw)
+
+        nc.scalar.activation(out=gm_neg[:], in_=gm_t[:], func=COPY, scale=-1.0)
+        for t in range(PACK):
+            nc.scalar.activation(out=ym[t][:, :S], in_=y_ps[t][:], func=COPY, scale=gm_neg[:, t : t + 1])
+            nc.scalar.activation(out=ym[t ^ 1][:, S:], in_=y_ps[t][:], func=COPY, scale=gm_t[:, t : t + 1])
+
+        part = [sb("part%d" % t, [P, S], F32) for t in range(PACK)]
+        z = sb("z", [P, PACK, S], F32)
+
+        def z_second(t):
+            nc.vector.tensor_scalar(part[t][:], yn[t][:].indirect(n2_t[:]), 0.75, 0.0, MULT, ADD)
+
+        def z_first(t):
+            nc.vector.tensor_tensor(z[:, t, :], yn[t][:].indirect(n1_t[:]), part[t][:], ADD)
+
+        z_second(0)
+        for t in range(1, PACK):
+            z_second(t)
+            z_first(t - 1)
+        deal(nc, w23s, w23s_raw)
+        z_first(PACK - 1)
+
+        z_grp = sb("z_grp", [P, S * PACK], BF16)
+        zw = sb("zw", [P, S], U32)
+        zs = sb("zs", [P, S], U8)
+        interleave(nc, z_grp, z)
+
+        z2 = [sb("z2_0", [P, PACK, HALF], F32)]
+        z2_grp = [sb("z2_grp%d" % h, [P, HALF * PACK], BF16) for h in range(2)]
+        z2w = [sb("z2w%d" % h, [P, HALF], U32) for h in range(2)]
+        z2s = [sb("z2s%d" % h, [P, HALF], U8) for h in range(2)]
+
+        def z2_gather(h, t):
+            nc.vector.tensor_tensor(
+                z2[h][:, t, :],
+                ym[t][:].indirect(n3_t[:, h * HALF // 16 : (h + 1) * HALF // 16]),
+                ym[t ^ 1][:, S + h * HALF : S + (h + 1) * HALF],
+                ADD,
+            )
+
+        a_ps = [psum.tile([P, S], F32, name="ab%d" % t) for t in range(PACK)]
+        b_ps = [psum.tile([P, S], F32, name="yb%d" % t) for t in range(PACK)]
+        a_sb = [sb("a_sb%d" % t, [P, S], F32) for t in range(PACK)]
+        b_sb = [sb("b_sb%d" % t, [P, S], F32) for t in range(PACK)]
+
+        def b_half(h):
+            nc.vector.quantize_mx(out=z2w[h][:].bitcast(FP8X4), scales=z2s[h][:], in_=z2_grp[h][:])
+            for t in range(PACK):
+                cols = slice(P * t, P * (t + 1))
+                nc.tensor.matmul_mx(
+                    out=b_ps[t][:, h * HALF : (h + 1) * HALF],
+                    lhsT=w3w[:, cols].bitcast(FP8X4),
+                    lhsT_scale=w23s[4:P, cols],
+                    rhs=z2w[h][:].bitcast(FP8X4),
+                    rhs_scale=z2s[h][:],
+                    start=True,
+                    stop=True,
+                )
+
+        for t in range(PACK):
+            z2_gather(0, t)
+        interleave(nc, z2_grp[0], z2[0])
+        nc.vector.quantize_mx(out=zw[:].bitcast(FP8X4), scales=zs[:], in_=z_grp[:])
+        for t in range(PACK):
+            cols = slice(P * t, P * (t + 1))
+            nc.tensor.matmul_mx(
+                out=a_ps[t][:], lhsT=w2w[:, cols].bitcast(FP8X4), lhsT_scale=w23s[:, cols], rhs=zw[:].bitcast(FP8X4), rhs_scale=zs[:], start=True, stop=True
+            )
+            nc.scalar.activation(out=a_sb[t][:], in_=a_ps[t][:], func=COPY)
+        z2.append(sb("z2_1", [P, PACK, HALF], F32, tag="z_grp"))
+        for t in range(PACK):
+            z2_gather(1, t)
+        interleave(nc, z2_grp[1], z2[1])
+        b_half(0)
+
+        a_half = [sb("a_half%d" % t, [P, W], F32) for t in range(2)]
+        b_got = [sb("b_got%d" % t, [P, W], F32) for t in range(PACK)]
+
+        def a_gather(t):
+            nc.vector.tensor_scalar(a_half[t][:], a_sb[t][:].indirect(n4_t[:]), -0.5, 0.0, MULT, ADD)
+
+        a_gather(0)
+        a_gather(1)
+        nc.scalar.activation(out=b_sb[0][:, :HALF], in_=b_ps[0][:, :HALF], func=COPY)
+        b_half(1)
+        a_half.append(sb("a_half2", [P, W], F32, tag="z2_grp1"))
+        a_half.append(sb("a_half3", [P, W], F32))
+        a_gather(2)
+        a_gather(3)
+        nc.scalar.activation(out=b_sb[0][:, HALF:], in_=b_ps[0][:, HALF:], func=COPY)
+        for t in range(1, PACK):
+            nc.scalar.activation(out=b_sb[t][:], in_=b_ps[t][:], func=COPY)
+
+        o_grp = [sb("o_grp%d" % h, [P, HALF, PACK], BF16) for h in range(2)]
+        ow = sb("ow", [P, S], I32)
+        osc = sb("osc", [P, S], U8)
+        rows_out = out_0.rearrange("(p t) c -> p t c", t=PACK)
+
+        nc.vector.tensor_copy(b_got[0][:], b_sb[0][:].indirect(n5_t[:]))
+        for t in range(PACK):
+            if t + 1 < PACK:
+                nc.vector.tensor_copy(b_got[t + 1][:], b_sb[t + 1][:].indirect(n5_t[:]))
+            nc.vector.tensor_tensor(a_sb[t][:].indirect(n4_t[:]), b_got[t][:], a_half[t][:], ADD)
+            nc.sync.dma_start(out=rows_out[:, t, :], in_=a_sb[t][:])
+            if t < 2:
+                nc.scalar.activation(out=o_grp[0][:, :, t], in_=a_sb[t][:, :HALF], func=COPY)
+            else:
+                nc.vector.tensor_copy(out=o_grp[0][:, :, t], in_=a_sb[t][:, :HALF])
+            nc.scalar.activation(out=o_grp[1][:, :, t], in_=a_sb[t][:, HALF:], func=COPY)
+
+        words_out = out_1[0].rearrange("p n t -> p (n t)").bitcast(I32)
+        for h in range(2):
+            cols = slice(h * HALF, (h + 1) * HALF)
+            nc.vector.quantize_mx(out=ow[:, cols].bitcast(FP8X4), scales=osc[:, cols], in_=o_grp[h][:].rearrange("p c t -> p (c t)"))
+            nc.sync.dma_start(out=words_out[:, cols], in_=ow[:, cols])
+        for q in range(4):
+            queue = nc.scalar if q % 2 else nc.sync
+            queue.dma_start(out=out_2[0, 4 * q : 4 * q + 4, :].bitcast(I32), in_=osc[32 * q : 32 * q + 4, :].bitcast(I32))

@@ -31,8 +31,11 @@ def load_words(nc, tile, words):
     nc.sync.dma_start(out=tile[:], in_=words[0].rearrange("p n t -> p (n t)").bitcast(I32))
 
 
-def deal(nc, dealt, raw):
-    nc.vector.tensor_copy(out=dealt[:].rearrange("p (t m) -> p t m", t=PACK), in_=raw[:].rearrange("p (m t) -> p t m", t=PACK))
+def deal(engine, dealt, raw, run, t0, t1):
+    engine.tensor_copy(
+        out=dealt[:].rearrange("p (t c i) -> p c t i", t=PACK, i=run)[:, :, t0:t1, :],
+        in_=raw[:].rearrange("p (c i t) -> p c t i", t=PACK, i=run)[:, :, t0:t1, :],
+    )
 
 
 def interleave(nc, grouped, rows):
@@ -88,14 +91,14 @@ def tile_picked_forkputbsumdif_none_po_kernel(
         nc.sync.dma_start(out=xw_raw[:, X_EARLY:], in_=x_flat[:, X_EARLY:])
         load_words(nc, w1w_raw, w1_words)
         load_scales(nc, w1s_raw, w1_scales, 0)
-        load_words(nc, w2w_raw, w2_words)
-        load_words(nc, w3w_raw, w3_words)
         nc.sync.dma_start(out=gn_t[:], in_=gn.rearrange("(p t) o -> p (t o)", t=PACK))
         nc.sync.dma_start(n2_t[:], n2)
-        nc.sync.dma_start(n1_t[:], n1)
         nc.sync.dma_start(out=gm_t[:], in_=gm.rearrange("(p t) o -> p (t o)", t=PACK))
-        nc.sync.dma_start(n3_t[:], n3)
+        load_words(nc, w2w_raw, w2_words)
+        load_words(nc, w3w_raw, w3_words)
         load_scales(nc, w23s_raw, w2_scales, 0)
+        nc.sync.dma_start(n1_t[:], n1)
+        nc.sync.dma_start(n3_t[:], n3)
         load_scales(nc, w23s_raw, w3_scales, 4)
         nc.sync.dma_start(n4_t[:], n4)
         nc.sync.dma_start(n5_t[:], n5)
@@ -109,30 +112,31 @@ def tile_picked_forkputbsumdif_none_po_kernel(
         w3w = sb("w3w", [P, N], I32)
 
         nc.vector.tensor_copy(xs[:], xs_raw[:].indirect(offs_t[:]))
-        nc.vector.tensor_copy(xw[:], xw_raw[:].bitcast(U32).indirect(offs_t[:]))
-        w1w_by_t = w1w_raw[:].rearrange("p (m t) -> p t m", t=PACK)
-        w1s_by_t = w1s_raw[:].rearrange("p (m t) -> p t m", t=PACK)
-        nc.vector.tensor_copy(out=w1w[:, :P], in_=w1w_by_t[:, 0, :])
-        nc.vector.tensor_copy(out=w1s[:, :P], in_=w1s_by_t[:, 0, :])
-        nc.vector.tensor_copy(out=w1s[:, P:].rearrange("p (t m) -> p t m", m=P), in_=w1s_by_t[:, 1:, :])
-        nc.vector.tensor_copy(out=w1w[:, P:].rearrange("p (t m) -> p t m", m=P), in_=w1w_by_t[:, 1:, :])
+        for h in range(2):
+            nc.vector.tensor_copy(xw[:, h * HALF : (h + 1) * HALF], xw_raw[:].bitcast(U32).indirect(offs_t[:, h * HALF // 16 : (h + 1) * HALF // 16]))
+        deal(nc.gpsimd, w1w, w1w_raw, 4, 0, 1)
+        deal(nc.gpsimd, w1s, w1s_raw, 16, 0, 1)
+        deal(nc.vector, w1w, w1w_raw, 4, 1, PACK)
+        deal(nc.vector, w1s, w1s_raw, 16, 1, PACK)
+        deal(nc.gpsimd, w2w, w2w_raw, 4, 0, PACK)
+        deal(nc.gpsimd, w3w, w3w_raw, 4, 0, PACK)
+        deal(nc.gpsimd, w23s, w23s_raw, 16, 0, PACK)
 
         y_ps = [psum.tile([P, S], F32, name="yb%d" % t) for t in range(PACK)]
-        for t in range(PACK):
+        y0_hi = psum.tile([P, HALF], F32, name="ab0")
+        pieces = [(0, 0, HALF, y_ps[0][:, :HALF]), (0, HALF, S, y0_hi[:])] + [(t, 0, S, y_ps[t][:]) for t in range(1, PACK)]
+        for t, c0, c1, bank in pieces:
             cols = slice(P * t, P * (t + 1))
             nc.tensor.matmul_mx(
-                out=y_ps[t][:], lhsT=w1w[:, cols].bitcast(FP8X4), lhsT_scale=w1s[:, cols], rhs=xw[:].bitcast(FP8X4), rhs_scale=xs[:], start=True, stop=True
+                out=bank, lhsT=w1w[:, cols].bitcast(FP8X4), lhsT_scale=w1s[:, cols], rhs=xw[:, c0:c1].bitcast(FP8X4), rhs_scale=xs[:, c0:c1], start=True, stop=True
             )
-        for t in range(PACK):
-            nc.scalar.activation(out=yn[t][:, :S], in_=y_ps[t][:], func=COPY, scale=gn_t[:, t : t + 1])
-
-        deal(nc, w2w, w2w_raw)
-        deal(nc, w3w, w3w_raw)
+        for t, c0, c1, bank in pieces:
+            nc.scalar.activation(out=yn[t][:, c0:c1], in_=bank, func=COPY, scale=gn_t[:, t : t + 1])
 
         nc.scalar.activation(out=gm_neg[:], in_=gm_t[:], func=COPY, scale=-1.0)
-        for t in range(PACK):
-            nc.scalar.activation(out=ym[t][:, :S], in_=y_ps[t][:], func=COPY, scale=gm_neg[:, t : t + 1])
-            nc.scalar.activation(out=ym[t ^ 1][:, S:], in_=y_ps[t][:], func=COPY, scale=gm_t[:, t : t + 1])
+        for t, c0, c1, bank in pieces:
+            nc.scalar.activation(out=ym[t][:, c0:c1], in_=bank, func=COPY, scale=gm_neg[:, t : t + 1])
+            nc.scalar.activation(out=ym[t ^ 1][:, S + c0 : S + c1], in_=bank, func=COPY, scale=gm_t[:, t : t + 1])
 
         part = [sb("part%d" % t, [P, S], F32) for t in range(PACK)]
         z = sb("z", [P, PACK, S], F32)
@@ -143,12 +147,10 @@ def tile_picked_forkputbsumdif_none_po_kernel(
         def z_first(t):
             nc.vector.tensor_tensor(z[:, t, :], yn[t][:].indirect(n1_t[:]), part[t][:], ADD)
 
-        z_second(0)
-        for t in range(1, PACK):
+        for t in range(PACK):
             z_second(t)
-            z_first(t - 1)
-        deal(nc, w23s, w23s_raw)
-        z_first(PACK - 1)
+        for t in range(PACK):
+            z_first(t)
 
         z_grp = sb("z_grp", [P, S * PACK], BF16)
         zw = sb("zw", [P, S], U32)

@@ -90,46 +90,51 @@ def tile_picked_forkputbsumdif_none_po_kernel(
         load_scales(nc, xs_raw, x_scales, 0)
         nc.sync.dma_start(out=xw_raw[:, X_EARLY:], in_=x_flat[:, X_EARLY:])
         load_words(nc, w1w_raw, w1_words)
-        load_scales(nc, w1s_raw, w1_scales, 0)
+        load_scales(nc, w1s_raw, w1_scales, 4)
         nc.sync.dma_start(out=gn_t[:], in_=gn.rearrange("(p t) o -> p (t o)", t=PACK))
-        nc.sync.dma_start(n2_t[:], n2)
-        nc.sync.dma_start(out=gm_t[:], in_=gm.rearrange("(p t) o -> p (t o)", t=PACK))
         load_words(nc, w2w_raw, w2_words)
         load_words(nc, w3w_raw, w3_words)
-        load_scales(nc, w23s_raw, w2_scales, 0)
+        nc.sync.dma_start(n2_t[:], n2)
+        nc.sync.dma_start(out=gm_t[:], in_=gm.rearrange("(p t) o -> p (t o)", t=PACK))
+        load_scales(nc, w23s_raw, w2_scales, 8)
         nc.sync.dma_start(n1_t[:], n1)
         nc.sync.dma_start(n3_t[:], n3)
-        load_scales(nc, w23s_raw, w3_scales, 4)
+        load_scales(nc, w23s_raw, w3_scales, 12)
         nc.sync.dma_start(n4_t[:], n4)
         nc.sync.dma_start(n5_t[:], n5)
 
         xs = sb("xs", [P, S], U8)
-        xw = sb("xw", [P, S], U32)
         w1s = sb("w1s", [P, H], U8)
         w1w = sb("w1w", [P, H], I32)
-        w23s = sb("w23s", [P, N], U8)
         w2w = sb("w2w", [P, N], I32)
         w3w = sb("w3w", [P, N], I32)
 
         nc.vector.tensor_copy(xs[:], xs_raw[:].indirect(offs_t[:]))
-        for h in range(2):
-            nc.vector.tensor_copy(xw[:, h * HALF : (h + 1) * HALF], xw_raw[:].bitcast(U32).indirect(offs_t[:, h * HALF // 16 : (h + 1) * HALF // 16]))
-        deal(nc.gpsimd, w1w, w1w_raw, 4, 0, 1)
-        deal(nc.gpsimd, w1s, w1s_raw, 16, 0, 1)
-        deal(nc.vector, w1w, w1w_raw, 4, 1, PACK)
-        deal(nc.vector, w1s, w1s_raw, 16, 1, PACK)
-        deal(nc.gpsimd, w2w, w2w_raw, 4, 0, PACK)
-        deal(nc.gpsimd, w3w, w3w_raw, 4, 0, PACK)
-        deal(nc.gpsimd, w23s, w23s_raw, 16, 0, PACK)
+        xw = [sb("xw0", [P, HALF], U32)]
+        nc.vector.tensor_copy(xw[0][:], xw_raw[:].bitcast(U32).indirect(offs_t[:, : HALF // 16]))
+        deal(nc.vector, w1w, w1w_raw, 4, 0, PACK)
+        deal(nc.vector, w1s, w1s_raw, 16, 0, PACK)
+        xw.append(sb("xw1", [P, HALF], U32, tag="w1s_raw"))
+        nc.vector.tensor_copy(xw[1][:], xw_raw[:].bitcast(U32).indirect(offs_t[:, HALF // 16 :]))
+        deal(nc.vector, w2w, w2w_raw, 4, 0, PACK)
+        deal(nc.vector, w3w, w3w_raw, 4, 0, PACK)
 
         y_ps = [psum.tile([P, S], F32, name="yb%d" % t) for t in range(PACK)]
         y0_hi = psum.tile([P, HALF], F32, name="ab0")
         pieces = [(0, 0, HALF, y_ps[0][:, :HALF]), (0, HALF, S, y0_hi[:])] + [(t, 0, S, y_ps[t][:]) for t in range(1, PACK)]
-        for t, c0, c1, bank in pieces:
+        for t in range(PACK):
             cols = slice(P * t, P * (t + 1))
-            nc.tensor.matmul_mx(
-                out=bank, lhsT=w1w[:, cols].bitcast(FP8X4), lhsT_scale=w1s[:, cols], rhs=xw[:, c0:c1].bitcast(FP8X4), rhs_scale=xs[:, c0:c1], start=True, stop=True
-            )
+            for h in range(2):
+                half = slice(h * HALF, (h + 1) * HALF)
+                nc.tensor.matmul_mx(
+                    out=y0_hi[:] if (t, h) == (0, 1) else y_ps[t][:, half],
+                    lhsT=w1w[:, cols].bitcast(FP8X4),
+                    lhsT_scale=w1s[4:P, cols],
+                    rhs=xw[h][:].bitcast(FP8X4),
+                    rhs_scale=xs[:, half],
+                    start=True,
+                    stop=True,
+                )
         for t, c0, c1, bank in pieces:
             nc.scalar.activation(out=yn[t][:, c0:c1], in_=bank, func=COPY, scale=gn_t[:, t : t + 1])
 
@@ -159,7 +164,6 @@ def tile_picked_forkputbsumdif_none_po_kernel(
 
         z2 = [sb("z2_0", [P, PACK, HALF], F32)]
         z2_grp = [sb("z2_grp%d" % h, [P, HALF * PACK], BF16) for h in range(2)]
-        z2w = [sb("z2w%d" % h, [P, HALF], U32) for h in range(2)]
         z2s = [sb("z2s%d" % h, [P, HALF], U8) for h in range(2)]
 
         def z2_gather(h, t):
@@ -182,7 +186,7 @@ def tile_picked_forkputbsumdif_none_po_kernel(
                 nc.tensor.matmul_mx(
                     out=b_ps[t][:, h * HALF : (h + 1) * HALF],
                     lhsT=w3w[:, cols].bitcast(FP8X4),
-                    lhsT_scale=w23s[4:P, cols],
+                    lhsT_scale=w23s[12:P, cols],
                     rhs=z2w[h][:].bitcast(FP8X4),
                     rhs_scale=z2s[h][:],
                     start=True,
@@ -192,17 +196,21 @@ def tile_picked_forkputbsumdif_none_po_kernel(
         for t in range(PACK):
             z2_gather(0, t)
         interleave(nc, z2_grp[0], z2[0])
+        w23s = sb("w23s", [P, N], U8, tag="part3")
+        deal(nc.vector, w23s, w23s_raw, 16, 0, PACK)
         nc.vector.quantize_mx(out=zw[:].bitcast(FP8X4), scales=zs[:], in_=z_grp[:])
         for t in range(PACK):
             cols = slice(P * t, P * (t + 1))
             nc.tensor.matmul_mx(
-                out=a_ps[t][:], lhsT=w2w[:, cols].bitcast(FP8X4), lhsT_scale=w23s[:, cols], rhs=zw[:].bitcast(FP8X4), rhs_scale=zs[:], start=True, stop=True
+                out=a_ps[t][:], lhsT=w2w[:, cols].bitcast(FP8X4), lhsT_scale=w23s[8:P, cols], rhs=zw[:].bitcast(FP8X4), rhs_scale=zs[:], start=True, stop=True
             )
-            nc.scalar.activation(out=a_sb[t][:], in_=a_ps[t][:], func=COPY)
+            if t + 1 < PACK:
+                nc.scalar.activation(out=a_sb[t][:], in_=a_ps[t][:], func=COPY)
         z2.append(sb("z2_1", [P, PACK, HALF], F32, tag="z_grp"))
         for t in range(PACK):
             z2_gather(1, t)
         interleave(nc, z2_grp[1], z2[1])
+        z2w = [sb("z2w0", [P, HALF], U32, tag="ym2"), sb("z2w1", [P, HALF], U32)]
         b_half(0)
 
         a_half = [sb("a_half%d" % t, [P, W], F32) for t in range(2)]
@@ -214,6 +222,7 @@ def tile_picked_forkputbsumdif_none_po_kernel(
         a_gather(0)
         a_gather(1)
         nc.scalar.activation(out=b_sb[0][:, :HALF], in_=b_ps[0][:, :HALF], func=COPY)
+        nc.scalar.activation(out=a_sb[PACK - 1][:], in_=a_ps[PACK - 1][:], func=COPY)
         b_half(1)
         a_half.append(sb("a_half2", [P, W], F32, tag="z2_grp1"))
         a_half.append(sb("a_half3", [P, W], F32))

@@ -17,33 +17,57 @@ MULT = mybir.AluOpType.mult
 ADD = mybir.AluOpType.add
 
 P = 128
-PACK = 4
+SLOTS = 4
+LAST = SLOTS - 1
 HALF = S // 2
+LIST_ROWS = 16
+QUADRANT = 32
+LINE_BYTES = 16
 X_EARLY = 768
+W1_FIRST, W2_FIRST, W3_FIRST = 4, 8, 12
 
 
-def load_scales(nc, plane, scales, first):
-    for q in range(4):
-        nc.sync.dma_start(out=plane[32 * q + first : 32 * q + first + 4, :].bitcast(I32), in_=scales[0, 4 * q : 4 * q + 4, :].bitcast(I32))
+def load_scales(nc, tile, scales, first):
+    for r in range(4):
+        nc.sync.dma_start(out=tile[first + r : P : QUADRANT, :].bitcast(I32), in_=scales[0, r::4, :].bitcast(I32))
 
 
-def load_words(nc, tile, words):
-    nc.sync.dma_start(out=tile[:], in_=words[0].rearrange("p n t -> p (n t)").bitcast(I32))
+def word_view(words):
+    return words[0].rearrange("p n t -> p (n t)").bitcast(I32)
 
 
-def deal(engine, dealt, raw, run, t0, t1):
-    engine.tensor_copy(
-        out=dealt[:].rearrange("p (t c i) -> p c t i", t=PACK, i=run)[:, :, t0:t1, :],
-        in_=raw[:].rearrange("p (c i t) -> p c t i", t=PACK, i=run)[:, :, t0:t1, :],
+def deal(nc, dealt, raw, run, first_slot=0, end_slot=SLOTS):
+    nc.vector.tensor_copy(
+        out=dealt.rearrange("p (t c i) -> p c t i", t=end_slot - first_slot, i=run),
+        in_=raw.rearrange("p (c i t) -> p c t i", t=SLOTS, i=run)[:, :, first_slot:end_slot, :],
     )
 
 
-def interleave(nc, grouped, rows):
+def interleave(nc, grouped, slots):
+    run = LINE_BYTES // 4
     nc.scalar.activation(
-        out=grouped[:].rearrange("p (c i t) -> p c t i", i=4, t=PACK),
-        in_=rows[:].rearrange("p t (c i) -> p c t i", i=4),
+        out=grouped.rearrange("p (c i t) -> p c t i", i=run, t=SLOTS),
+        in_=slots.rearrange("p t (c i) -> p c t i", i=run),
         func=COPY,
     )
+
+
+def product(nc, out, weight_words, weight_scales, words, scales):
+    nc.tensor.matmul_mx(
+        out=out, lhsT=weight_words.bitcast(FP8X4), lhsT_scale=weight_scales, rhs=words.bitcast(FP8X4), rhs_scale=scales, start=True, stop=True
+    )
+
+
+def half_cols(h):
+    return slice(h * HALF, (h + 1) * HALF)
+
+
+def half_list(tile, h):
+    return tile[:, h * HALF // LIST_ROWS : (h + 1) * HALF // LIST_ROWS]
+
+
+def slot_cols(t):
+    return slice(t * P, (t + 1) * P)
 
 
 def tile_picked_forkputbsumdif_none_po_kernel(
@@ -57,12 +81,12 @@ def tile_picked_forkputbsumdif_none_po_kernel(
         def sb(name, shape, dtype, tag=None):
             return keep.tile(shape, dtype, name=name, tag=tag or name, align_bytes=64)
 
-        offs_t = sb("offs_t", [P, S // 16], U16)
-        n1_t = sb("n1_t", [P, S // 16], U16)
-        n2_t = sb("n2_t", [P, S // 16], U16)
-        n3_t = sb("n3_t", [P, S // 16], U16)
-        n4_t = sb("n4_t", [P, W // 16], U16)
-        n5_t = sb("n5_t", [P, W // 16], U16)
+        offs_t = sb("offs_t", [P, S // LIST_ROWS], U16)
+        n1_t = sb("n1_t", [P, S // LIST_ROWS], U16)
+        n2_t = sb("n2_t", [P, S // LIST_ROWS], U16)
+        n3_t = sb("n3_t", [P, S // LIST_ROWS], U16)
+        n4_t = sb("n4_t", [P, W // LIST_ROWS], U16)
+        n5_t = sb("n5_t", [P, W // LIST_ROWS], U16)
 
         xs_raw = sb("xs_raw", [P, T], U8)
         xw_raw = sb("xw_raw", [P, T], I32)
@@ -71,189 +95,154 @@ def tile_picked_forkputbsumdif_none_po_kernel(
         w1w_raw = sb("w1w_raw", [P, H], I32)
         w2w_raw = sb("w2w_raw", [P, N], I32)
         w3w_raw = sb("w3w_raw", [P, N], I32)
-        gn_t = sb("gn_t", [P, PACK], F32)
-        gm_t = sb("gm_t", [P, PACK], F32)
-        gm_neg = sb("gm_neg", [P, PACK], F32)
-        yn = [sb("yn%d" % t, [P, 2 * S], F32) for t in range(PACK)]
-        ym = [sb("ym%d" % t, [P, 2 * S], F32) for t in range(PACK)]
+        gn_t = sb("gn_t", [P, SLOTS], F32)
+        gm_t = sb("gm_t", [P, SLOTS], F32)
+        gm_neg = sb("gm_neg", [P, SLOTS], F32)
+        yn = [sb("yn%d" % t, [P, 2 * S], F32) for t in range(SLOTS)]
+        ym = [sb("ym%d" % t, [P, 2 * S], F32) for t in range(SLOTS)]
 
         nc.vector.memset(xs_raw[:].bitcast(I32), 0)
         nc.vector.memset(w1s_raw[:].bitcast(I32), 0)
         nc.vector.memset(yn[0][:, S:], 0.0)
         nc.vector.memset(w23s_raw[:].bitcast(I32), 0)
-        for t in range(1, PACK):
+        for t in range(1, SLOTS):
             nc.scalar.activation(out=yn[t][:, S:], in_=yn[0][:, S:], func=COPY)
 
-        x_flat = x_words[0].rearrange("p n t -> p (n t)").bitcast(I32)
+        nc.sync.dma_start(out=xw_raw[:, :X_EARLY], in_=word_view(x_words)[:, :X_EARLY])
         nc.sync.dma_start(offs_t[:], offs)
-        nc.sync.dma_start(out=xw_raw[:, :X_EARLY], in_=x_flat[:, :X_EARLY])
         load_scales(nc, xs_raw, x_scales, 0)
-        nc.sync.dma_start(out=xw_raw[:, X_EARLY:], in_=x_flat[:, X_EARLY:])
-        load_words(nc, w1w_raw, w1_words)
-        load_scales(nc, w1s_raw, w1_scales, 4)
-        nc.sync.dma_start(out=gn_t[:], in_=gn.rearrange("(p t) o -> p (t o)", t=PACK))
-        load_words(nc, w2w_raw, w2_words)
-        load_words(nc, w3w_raw, w3_words)
+        nc.sync.dma_start(out=xw_raw[:, X_EARLY:], in_=word_view(x_words)[:, X_EARLY:])
+        nc.sync.dma_start(out=w1w_raw[:], in_=word_view(w1_words))
+        load_scales(nc, w1s_raw, w1_scales, W1_FIRST)
+        nc.sync.dma_start(out=gn_t[:], in_=gn.rearrange("(p t) o -> p (t o)", t=SLOTS))
+        nc.sync.dma_start(out=w2w_raw[:], in_=word_view(w2_words))
+        nc.sync.dma_start(out=w3w_raw[:], in_=word_view(w3_words))
         nc.sync.dma_start(n2_t[:], n2)
-        nc.sync.dma_start(out=gm_t[:], in_=gm.rearrange("(p t) o -> p (t o)", t=PACK))
-        load_scales(nc, w23s_raw, w2_scales, 8)
+        nc.sync.dma_start(out=gm_t[:], in_=gm.rearrange("(p t) o -> p (t o)", t=SLOTS))
+        load_scales(nc, w23s_raw, w2_scales, W2_FIRST)
         nc.sync.dma_start(n1_t[:], n1)
         nc.sync.dma_start(n3_t[:], n3)
-        load_scales(nc, w23s_raw, w3_scales, 12)
+        load_scales(nc, w23s_raw, w3_scales, W3_FIRST)
         nc.sync.dma_start(n4_t[:], n4)
         nc.sync.dma_start(n5_t[:], n5)
 
         xs = sb("xs", [P, S], U8)
         w1s = sb("w1s", [P, H], U8)
-        w1w = sb("w1w", [P, H], I32)
+        w1w_first = sb("w1w_first", [P, P], I32)
         w2w = sb("w2w", [P, N], I32)
         w3w = sb("w3w", [P, N], I32)
-
-        nc.vector.tensor_copy(xs[:], xs_raw[:].indirect(offs_t[:]))
         xw = [sb("xw0", [P, HALF], U32)]
-        nc.vector.tensor_copy(xw[0][:], xw_raw[:].bitcast(U32).indirect(offs_t[:, : HALF // 16]))
-        deal(nc.vector, w1w, w1w_raw, 4, 0, PACK)
-        deal(nc.vector, w1s, w1s_raw, 16, 0, PACK)
+        nc.vector.tensor_copy(xs[:], xs_raw[:].indirect(offs_t[:]))
+        nc.vector.tensor_copy(xw[0][:], xw_raw[:].bitcast(U32).indirect(half_list(offs_t, 0)))
+        deal(nc, w1w_first[:], w1w_raw[:], LINE_BYTES // 4, 0, 1)
+        deal(nc, w1s[:], w1s_raw[:], LINE_BYTES)
         xw.append(sb("xw1", [P, HALF], U32, tag="w1s_raw"))
-        nc.vector.tensor_copy(xw[1][:], xw_raw[:].bitcast(U32).indirect(offs_t[:, HALF // 16 :]))
-        deal(nc.vector, w2w, w2w_raw, 4, 0, PACK)
-        deal(nc.vector, w3w, w3w_raw, 4, 0, PACK)
+        nc.vector.tensor_copy(xw[1][:], xw_raw[:].bitcast(U32).indirect(half_list(offs_t, 1)))
+        w1w_rest = sb("w1w_rest", [P, H - P], I32, tag="xw_raw")
+        deal(nc, w1w_rest[:], w1w_raw[:], LINE_BYTES // 4, 1, SLOTS)
+        deal(nc, w2w[:], w2w_raw[:], LINE_BYTES // 4)
+        deal(nc, w3w[:], w3w_raw[:], LINE_BYTES // 4)
 
-        y_ps = [psum.tile([P, S], F32, name="yb%d" % t) for t in range(PACK)]
-        y0_hi = psum.tile([P, HALF], F32, name="ab0")
-        pieces = [(0, 0, HALF, y_ps[0][:, :HALF]), (0, HALF, S, y0_hi[:])] + [(t, 0, S, y_ps[t][:]) for t in range(1, PACK)]
-        for t in range(PACK):
-            cols = slice(P * t, P * (t + 1))
-            for h in range(2):
-                half = slice(h * HALF, (h + 1) * HALF)
-                nc.tensor.matmul_mx(
-                    out=y0_hi[:] if (t, h) == (0, 1) else y_ps[t][:, half],
-                    lhsT=w1w[:, cols].bitcast(FP8X4),
-                    lhsT_scale=w1s[4:P, cols],
-                    rhs=xw[h][:].bitcast(FP8X4),
-                    rhs_scale=xs[:, half],
-                    start=True,
-                    stop=True,
-                )
-        for t, c0, c1, bank in pieces:
-            nc.scalar.activation(out=yn[t][:, c0:c1], in_=bank, func=COPY, scale=gn_t[:, t : t + 1])
-
+        y_ps = [psum.tile([P, S], F32, name="yb%d" % t) for t in range(SLOTS)]
+        y0_second = psum.tile([P, HALF], F32, name="ab0")
+        product(nc, y_ps[0][:, :HALF], w1w_first[:], w1s[W1_FIRST:P, slot_cols(0)], xw[0][:], xs[:, :HALF])
+        product(nc, y0_second[:], w1w_first[:], w1s[W1_FIRST:P, slot_cols(0)], xw[1][:], xs[:, HALF:])
+        for t in range(1, SLOTS):
+            for h in (1, 0):
+                product(nc, y_ps[t][:, half_cols(h)], w1w_rest[:, slot_cols(t - 1)], w1s[W1_FIRST:P, slot_cols(t)], xw[h][:], xs[:, half_cols(h)])
+        y_pieces = [(0, 0, HALF, y_ps[0][:, :HALF]), (0, HALF, S, y0_second[:])] + [(t, 0, S, y_ps[t][:]) for t in range(1, SLOTS)]
+        for t, c0, c1, piece in y_pieces:
+            nc.scalar.activation(out=yn[t][:, c0:c1], in_=piece, func=COPY, scale=gn_t[:, t : t + 1])
         nc.scalar.activation(out=gm_neg[:], in_=gm_t[:], func=COPY, scale=-1.0)
-        for t, c0, c1, bank in pieces:
-            nc.scalar.activation(out=ym[t][:, c0:c1], in_=bank, func=COPY, scale=gm_neg[:, t : t + 1])
-            nc.scalar.activation(out=ym[t ^ 1][:, S + c0 : S + c1], in_=bank, func=COPY, scale=gm_t[:, t : t + 1])
+        for t, c0, c1, piece in y_pieces:
+            nc.scalar.activation(out=ym[t][:, c0:c1], in_=piece, func=COPY, scale=gm_neg[:, t : t + 1])
+            nc.scalar.activation(out=ym[t ^ 1][:, S + c0 : S + c1], in_=piece, func=COPY, scale=gm_t[:, t : t + 1])
 
-        part = [sb("part%d" % t, [P, S], F32) for t in range(PACK)]
-        z = sb("z", [P, PACK, S], F32)
-
-        def z_second(t):
-            nc.vector.tensor_scalar(part[t][:], yn[t][:].indirect(n2_t[:]), 0.75, 0.0, MULT, ADD)
-
-        def z_first(t):
-            nc.vector.tensor_tensor(z[:, t, :], yn[t][:].indirect(n1_t[:]), part[t][:], ADD)
-
-        for t in range(PACK):
-            z_second(t)
-        for t in range(PACK):
-            z_first(t)
-
-        z_grp = sb("z_grp", [P, S * PACK], BF16)
+        z_term = [sb("z_term%d" % t, [P, S], F32) for t in range(SLOTS)]
+        z = sb("z", [P, SLOTS, S], F32)
+        for t in range(SLOTS):
+            nc.vector.tensor_scalar(z_term[t][:], yn[t][:].indirect(n2_t[:]), 0.75, 0.0, MULT, ADD)
+        for t in range(SLOTS):
+            nc.vector.tensor_tensor(z[:, t, :], yn[t][:].indirect(n1_t[:]), z_term[t][:], ADD)
+        z_grouped = sb("z_grouped", [P, S * SLOTS], BF16)
         zw = sb("zw", [P, S], U32)
         zs = sb("zs", [P, S], U8)
-        interleave(nc, z_grp, z)
+        interleave(nc, z_grouped[:], z[:])
 
-        z2 = [sb("z2_0", [P, PACK, HALF], F32)]
-        z2_grp = [sb("z2_grp%d" % h, [P, HALF * PACK], BF16) for h in range(2)]
+        z2 = [sb("z2_0", [P, SLOTS, HALF], F32)]
+        z2_grouped = [sb("z2_grouped%d" % h, [P, HALF * SLOTS], BF16) for h in range(2)]
         z2s = [sb("z2s%d" % h, [P, HALF], U8) for h in range(2)]
 
-        def z2_gather(h, t):
-            nc.vector.tensor_tensor(
-                z2[h][:, t, :],
-                ym[t][:].indirect(n3_t[:, h * HALF // 16 : (h + 1) * HALF // 16]),
-                ym[t ^ 1][:, S + h * HALF : S + (h + 1) * HALF],
-                ADD,
-            )
+        def z2_half(h):
+            for t in range(SLOTS):
+                plain = ym[t ^ 1][:, S + h * HALF : S + (h + 1) * HALF]
+                nc.vector.tensor_tensor(z2[h][:, t, :], ym[t][:].indirect(half_list(n3_t, h)), plain, ADD)
 
-        a_ps = [psum.tile([P, S], F32, name="ab%d" % t) for t in range(PACK)]
-        b_ps = [psum.tile([P, S], F32, name="yb%d" % t) for t in range(PACK)]
-        a_sb = [sb("a_sb%d" % t, [P, S], F32) for t in range(PACK)]
-        b_sb = [sb("b_sb%d" % t, [P, S], F32) for t in range(PACK)]
+        a_ps = [psum.tile([P, S], F32, name="ab%d" % t) for t in range(SLOTS)]
+        b_ps = [psum.tile([P, S], F32, name="yb%d" % t) for t in range(SLOTS)]
+        a_sb = [sb("a_sb%d" % t, [P, S], F32) for t in range(SLOTS)]
+        b_sb = [sb("b_sb%d" % t, [P, S], F32) for t in range(SLOTS)]
+
+        z2_half(0)
+        interleave(nc, z2_grouped[0][:], z2[0][:])
+        w23s = sb("w23s", [P, N], U8, tag="z_term%d" % LAST)
+        deal(nc, w23s[:], w23s_raw[:], LINE_BYTES)
+        nc.vector.quantize_mx(out=zw[:].bitcast(FP8X4), scales=zs[:], in_=z_grouped[:])
+        for t in range(SLOTS):
+            product(nc, a_ps[t][:], w2w[:, slot_cols(t)], w23s[W2_FIRST:P, slot_cols(t)], zw[:], zs[:])
+            if t < LAST:
+                nc.scalar.activation(out=a_sb[t][:], in_=a_ps[t][:], func=COPY)
+        z2.append(sb("z2_1", [P, SLOTS, HALF], F32, tag="z_grouped"))
+        z2_half(1)
+        interleave(nc, z2_grouped[1][:], z2[1][:])
+
+        z2w = [sb("z2w0", [P, HALF], U32, tag="ym%d" % (LAST ^ 1)), sb("z2w1", [P, HALF], U32)]
 
         def b_half(h):
-            nc.vector.quantize_mx(out=z2w[h][:].bitcast(FP8X4), scales=z2s[h][:], in_=z2_grp[h][:])
-            for t in range(PACK):
-                cols = slice(P * t, P * (t + 1))
-                nc.tensor.matmul_mx(
-                    out=b_ps[t][:, h * HALF : (h + 1) * HALF],
-                    lhsT=w3w[:, cols].bitcast(FP8X4),
-                    lhsT_scale=w23s[12:P, cols],
-                    rhs=z2w[h][:].bitcast(FP8X4),
-                    rhs_scale=z2s[h][:],
-                    start=True,
-                    stop=True,
-                )
-
-        for t in range(PACK):
-            z2_gather(0, t)
-        interleave(nc, z2_grp[0], z2[0])
-        w23s = sb("w23s", [P, N], U8, tag="part3")
-        deal(nc.vector, w23s, w23s_raw, 16, 0, PACK)
-        nc.vector.quantize_mx(out=zw[:].bitcast(FP8X4), scales=zs[:], in_=z_grp[:])
-        for t in range(PACK):
-            cols = slice(P * t, P * (t + 1))
-            nc.tensor.matmul_mx(
-                out=a_ps[t][:], lhsT=w2w[:, cols].bitcast(FP8X4), lhsT_scale=w23s[8:P, cols], rhs=zw[:].bitcast(FP8X4), rhs_scale=zs[:], start=True, stop=True
-            )
-            if t + 1 < PACK:
-                nc.scalar.activation(out=a_sb[t][:], in_=a_ps[t][:], func=COPY)
-        z2.append(sb("z2_1", [P, PACK, HALF], F32, tag="z_grp"))
-        for t in range(PACK):
-            z2_gather(1, t)
-        interleave(nc, z2_grp[1], z2[1])
-        z2w = [sb("z2w0", [P, HALF], U32, tag="ym2"), sb("z2w1", [P, HALF], U32)]
-        b_half(0)
-
-        a_half = [sb("a_half%d" % t, [P, W], F32) for t in range(2)]
-        b_got = [sb("b_got%d" % t, [P, W], F32) for t in range(PACK)]
+            nc.vector.quantize_mx(out=z2w[h][:].bitcast(FP8X4), scales=z2s[h][:], in_=z2_grouped[h][:])
+            for t in range(SLOTS):
+                product(nc, b_ps[t][:, half_cols(h)], w3w[:, slot_cols(t)], w23s[W3_FIRST:P, slot_cols(t)], z2w[h][:], z2s[h][:])
 
         def a_gather(t):
-            nc.vector.tensor_scalar(a_half[t][:], a_sb[t][:].indirect(n4_t[:]), -0.5, 0.0, MULT, ADD)
+            nc.vector.tensor_scalar(a_term[t][:], a_sb[t][:].indirect(n4_t[:]), -0.5, 0.0, MULT, ADD)
 
+        b_half(0)
+        a_term = [sb("a_term%d" % t, [P, W], F32) for t in range(2)]
+        b_term = [sb("b_term%d" % t, [P, W], F32) for t in range(SLOTS)]
         a_gather(0)
         a_gather(1)
         nc.scalar.activation(out=b_sb[0][:, :HALF], in_=b_ps[0][:, :HALF], func=COPY)
-        nc.scalar.activation(out=a_sb[PACK - 1][:], in_=a_ps[PACK - 1][:], func=COPY)
+        nc.scalar.activation(out=a_sb[LAST][:], in_=a_ps[LAST][:], func=COPY)
         b_half(1)
-        a_half.append(sb("a_half2", [P, W], F32, tag="z2_grp1"))
-        a_half.append(sb("a_half3", [P, W], F32))
+        a_term.append(sb("a_term2", [P, W], F32, tag="z2_grouped1"))
+        a_term.append(sb("a_term3", [P, W], F32))
         a_gather(2)
         a_gather(3)
         nc.scalar.activation(out=b_sb[0][:, HALF:], in_=b_ps[0][:, HALF:], func=COPY)
-        for t in range(1, PACK):
+        for t in range(1, SLOTS):
             nc.scalar.activation(out=b_sb[t][:], in_=b_ps[t][:], func=COPY)
 
-        o_grp = [sb("o_grp%d" % h, [P, HALF, PACK], BF16) for h in range(2)]
-        ow = sb("ow", [P, S], I32)
-        osc = sb("osc", [P, S], U8)
-        rows_out = out_0.rearrange("(p t) c -> p t c", t=PACK)
+        out_grouped = [sb("out_grouped%d" % h, [P, HALF, SLOTS], BF16) for h in range(2)]
+        out_words = sb("out_words", [P, S], I32)
+        out_scales = sb("out_scales", [P, S], U8)
+        out_slots = out_0.rearrange("(p t) c -> p t c", t=SLOTS)
 
-        nc.vector.tensor_copy(b_got[0][:], b_sb[0][:].indirect(n5_t[:]))
-        for t in range(PACK):
-            if t + 1 < PACK:
-                nc.vector.tensor_copy(b_got[t + 1][:], b_sb[t + 1][:].indirect(n5_t[:]))
-            nc.vector.tensor_tensor(a_sb[t][:].indirect(n4_t[:]), b_got[t][:], a_half[t][:], ADD)
-            nc.sync.dma_start(out=rows_out[:, t, :], in_=a_sb[t][:])
-            if t < 2:
-                nc.scalar.activation(out=o_grp[0][:, :, t], in_=a_sb[t][:, :HALF], func=COPY)
+        nc.vector.tensor_copy(b_term[0][:], b_sb[0][:].indirect(n5_t[:]))
+        for t in range(SLOTS):
+            if t < LAST:
+                nc.vector.tensor_copy(b_term[t + 1][:], b_sb[t + 1][:].indirect(n5_t[:]))
+            nc.vector.tensor_tensor(a_sb[t][:].indirect(n4_t[:]), b_term[t][:], a_term[t][:], ADD)
+            nc.sync.dma_start(out=out_slots[:, t, :], in_=a_sb[t][:])
+            if t // 2 == LAST // 2:
+                nc.vector.tensor_copy(out=out_grouped[0][:, :, t], in_=a_sb[t][:, :HALF])
             else:
-                nc.vector.tensor_copy(out=o_grp[0][:, :, t], in_=a_sb[t][:, :HALF])
-            nc.scalar.activation(out=o_grp[1][:, :, t], in_=a_sb[t][:, HALF:], func=COPY)
+                nc.scalar.activation(out=out_grouped[0][:, :, t], in_=a_sb[t][:, :HALF], func=COPY)
+            nc.scalar.activation(out=out_grouped[1][:, :, t], in_=a_sb[t][:, HALF:], func=COPY)
 
-        words_out = out_1[0].rearrange("p n t -> p (n t)").bitcast(I32)
         for h in range(2):
-            cols = slice(h * HALF, (h + 1) * HALF)
-            nc.vector.quantize_mx(out=ow[:, cols].bitcast(FP8X4), scales=osc[:, cols], in_=o_grp[h][:].rearrange("p c t -> p (c t)"))
-            nc.sync.dma_start(out=words_out[:, cols], in_=ow[:, cols])
-        for q in range(4):
-            queue = nc.scalar if q % 2 else nc.sync
-            queue.dma_start(out=out_2[0, 4 * q : 4 * q + 4, :].bitcast(I32), in_=osc[32 * q : 32 * q + 4, :].bitcast(I32))
+            grouped = out_grouped[h][:].rearrange("p c t -> p (c t)")
+            nc.vector.quantize_mx(out=out_words[:, half_cols(h)].bitcast(FP8X4), scales=out_scales[:, half_cols(h)], in_=grouped)
+            nc.sync.dma_start(out=word_view(out_1)[:, half_cols(h)], in_=out_words[:, half_cols(h)])
+        for r in range(4):
+            queue = nc.scalar if r % 2 else nc.sync
+            queue.dma_start(out=out_2[0, r::4, :].bitcast(I32), in_=out_scales[r:P:QUADRANT, :].bitcast(I32))

from contextlib import ExitStack

import concourse.mybir as mybir

K, T, S, N, H, W = 512, 2048, 512, 512, 512, 256
FLOPS = 2 * K * H * S + 2 * 2 * H * N * S

F32 = mybir.dt.float32
BF16 = mybir.dt.bfloat16
I32 = mybir.dt.int32
U32 = mybir.dt.uint32
U16 = mybir.dt.uint16
U8 = mybir.dt.uint8
FP8X4 = mybir.dt.float8_e4m3fn_x4
COPY = mybir.ActivationFunctionType.Copy
MULT = mybir.AluOpType.mult
ADD = mybir.AluOpType.add

P = 128
SLOTS = 4
LAST = SLOTS - 1
HALF = S // 2
LIST_ROWS = 16
QUADRANT = 32
LINE_BYTES = 16
X_EARLY = 768
W1_FIRST, W2_FIRST, W3_FIRST = 4, 8, 12


def load_scales(nc, tile, scales, first):
    for r in range(4):
        nc.sync.dma_start(out=tile[first + r : P : QUADRANT, :].bitcast(I32), in_=scales[0, r::4, :].bitcast(I32))


def word_view(words):
    return words[0].rearrange("p n t -> p (n t)").bitcast(I32)


def deal(nc, dealt, raw, run, first_slot=0, end_slot=SLOTS):
    nc.vector.tensor_copy(
        out=dealt.rearrange("p (t c i) -> p c t i", t=end_slot - first_slot, i=run),
        in_=raw.rearrange("p (c i t) -> p c t i", t=SLOTS, i=run)[:, :, first_slot:end_slot, :],
    )


def interleave(nc, grouped, slots):
    run = LINE_BYTES // 4
    nc.scalar.activation(
        out=grouped.rearrange("p (c i t) -> p c t i", i=run, t=SLOTS),
        in_=slots.rearrange("p t (c i) -> p c t i", i=run),
        func=COPY,
    )


def product(nc, out, weight_words, weight_scales, words, scales):
    nc.tensor.matmul_mx(
        out=out, lhsT=weight_words.bitcast(FP8X4), lhsT_scale=weight_scales, rhs=words.bitcast(FP8X4), rhs_scale=scales, start=True, stop=True
    )


def half_cols(h):
    return slice(h * HALF, (h + 1) * HALF)


def half_list(tile, h):
    return tile[:, h * HALF // LIST_ROWS : (h + 1) * HALF // LIST_ROWS]


def slot_cols(t):
    return slice(t * P, (t + 1) * P)


def tile_picked_forkputbsumdif_none_po_kernel(
    tc, x_words, x_scales, w1_words, w1_scales, gn, w2_words, w2_scales, gm, w3_words, w3_scales, offs, n1, n2, n3, n4, n5, out_0, out_1, out_2
):
    nc = tc.nc
    with ExitStack() as ctx:
        keep = ctx.enter_context(tc.tile_pool(name="keep", bufs=1))
        psum = ctx.enter_context(tc.psum_pool(name="psum", bufs=1))

        def sb(name, shape, dtype, tag=None):
            return keep.tile(shape, dtype, name=name, tag=tag or name, align_bytes=64)

        offs_t = sb("offs_t", [P, S // LIST_ROWS], U16)
        n1_t = sb("n1_t", [P, S // LIST_ROWS], U16)
        n2_t = sb("n2_t", [P, S // LIST_ROWS], U16)
        n3_t = sb("n3_t", [P, S // LIST_ROWS], U16)
        n4_t = sb("n4_t", [P, W // LIST_ROWS], U16)
        n5_t = sb("n5_t", [P, W // LIST_ROWS], U16)

        xs_raw = sb("xs_raw", [P, T], U8)
        xw_raw = sb("xw_raw", [P, T], I32)
        w1s_raw = sb("w1s_raw", [P, H], U8)
        w23s_raw = sb("w23s_raw", [P, N], U8)
        w1w_raw = sb("w1w_raw", [P, H], I32)
        w2w_raw = sb("w2w_raw", [P, N], I32)
        w3w_raw = sb("w3w_raw", [P, N], I32)
        gn_t = sb("gn_t", [P, SLOTS], F32)
        gm_t = sb("gm_t", [P, SLOTS], F32)
        gm_neg = sb("gm_neg", [P, SLOTS], F32)
        yn = [sb("yn%d" % t, [P, 2 * S], F32) for t in range(SLOTS)]
        ym = [sb("ym%d" % t, [P, 2 * S], F32) for t in range(SLOTS)]

        nc.vector.memset(xs_raw[:].bitcast(I32), 0)
        nc.vector.memset(w1s_raw[:].bitcast(I32), 0)
        nc.vector.memset(yn[0][:, S:], 0.0)
        nc.vector.memset(w23s_raw[:].bitcast(I32), 0)
        for t in range(1, SLOTS):
            nc.scalar.activation(out=yn[t][:, S:], in_=yn[0][:, S:], func=COPY)

        nc.sync.dma_start(out=xw_raw[:, :X_EARLY], in_=word_view(x_words)[:, :X_EARLY])
        nc.sync.dma_start(offs_t[:], offs)
        load_scales(nc, xs_raw, x_scales, 0)
        nc.sync.dma_start(out=xw_raw[:, X_EARLY:], in_=word_view(x_words)[:, X_EARLY:])
        nc.sync.dma_start(out=w1w_raw[:], in_=word_view(w1_words))
        load_scales(nc, w1s_raw, w1_scales, W1_FIRST)
        nc.sync.dma_start(out=gn_t[:], in_=gn.rearrange("(p t) o -> p (t o)", t=SLOTS))
        nc.sync.dma_start(out=w2w_raw[:], in_=word_view(w2_words))
        nc.sync.dma_start(out=w3w_raw[:], in_=word_view(w3_words))
        nc.sync.dma_start(n2_t[:], n2)
        nc.sync.dma_start(out=gm_t[:], in_=gm.rearrange("(p t) o -> p (t o)", t=SLOTS))
        load_scales(nc, w23s_raw, w2_scales, W2_FIRST)
        nc.sync.dma_start(n1_t[:], n1)
        nc.sync.dma_start(n3_t[:], n3)
        load_scales(nc, w23s_raw, w3_scales, W3_FIRST)
        nc.sync.dma_start(n4_t[:], n4)
        nc.sync.dma_start(n5_t[:], n5)

        xs = sb("xs", [P, S], U8)
        w1s = sb("w1s", [P, H], U8)
        w1w_first = sb("w1w_first", [P, P], I32)
        w2w = sb("w2w", [P, N], I32)
        w3w = sb("w3w", [P, N], I32)
        xw = [sb("xw0", [P, HALF], U32)]
        nc.vector.tensor_copy(xs[:], xs_raw[:].indirect(offs_t[:]))
        nc.vector.tensor_copy(xw[0][:], xw_raw[:].bitcast(U32).indirect(half_list(offs_t, 0)))
        deal(nc, w1w_first[:], w1w_raw[:], LINE_BYTES // 4, 0, 1)
        deal(nc, w1s[:], w1s_raw[:], LINE_BYTES)
        xw.append(sb("xw1", [P, HALF], U32, tag="w1s_raw"))
        nc.vector.tensor_copy(xw[1][:], xw_raw[:].bitcast(U32).indirect(half_list(offs_t, 1)))
        w1w_rest = sb("w1w_rest", [P, H - P], I32, tag="xw_raw")
        deal(nc, w1w_rest[:], w1w_raw[:], LINE_BYTES // 4, 1, SLOTS)
        deal(nc, w2w[:], w2w_raw[:], LINE_BYTES // 4)
        deal(nc, w3w[:], w3w_raw[:], LINE_BYTES // 4)

        y_ps = [psum.tile([P, S], F32, name="yb%d" % t) for t in range(SLOTS)]
        y0_second = psum.tile([P, HALF], F32, name="ab0")
        product(nc, y_ps[0][:, :HALF], w1w_first[:], w1s[W1_FIRST:P, slot_cols(0)], xw[0][:], xs[:, :HALF])
        product(nc, y0_second[:], w1w_first[:], w1s[W1_FIRST:P, slot_cols(0)], xw[1][:], xs[:, HALF:])
        for t in range(1, SLOTS):
            for h in (1, 0):
                product(nc, y_ps[t][:, half_cols(h)], w1w_rest[:, slot_cols(t - 1)], w1s[W1_FIRST:P, slot_cols(t)], xw[h][:], xs[:, half_cols(h)])
        y_pieces = [(0, 0, HALF, y_ps[0][:, :HALF]), (0, HALF, S, y0_second[:])] + [(t, 0, S, y_ps[t][:]) for t in range(1, SLOTS)]
        for t, c0, c1, piece in y_pieces:
            nc.scalar.activation(out=yn[t][:, c0:c1], in_=piece, func=COPY, scale=gn_t[:, t : t + 1])
        nc.scalar.activation(out=gm_neg[:], in_=gm_t[:], func=COPY, scale=-1.0)
        for t, c0, c1, piece in y_pieces:
            nc.scalar.activation(out=ym[t][:, c0:c1], in_=piece, func=COPY, scale=gm_neg[:, t : t + 1])
            nc.scalar.activation(out=ym[t ^ 1][:, S + c0 : S + c1], in_=piece, func=COPY, scale=gm_t[:, t : t + 1])

        z_term = [sb("z_term%d" % t, [P, S], F32) for t in range(SLOTS)]
        z = sb("z", [P, SLOTS, S], F32)
        for t in range(SLOTS):
            nc.vector.tensor_scalar(z_term[t][:], yn[t][:].indirect(n2_t[:]), 0.75, 0.0, MULT, ADD)
        for t in range(SLOTS):
            nc.vector.tensor_tensor(z[:, t, :], yn[t][:].indirect(n1_t[:]), z_term[t][:], ADD)
        z_grouped = sb("z_grouped", [P, S * SLOTS], BF16)
        zw = sb("zw", [P, S], U32)
        zs = sb("zs", [P, S], U8)
        interleave(nc, z_grouped[:], z[:])

        z2 = [sb("z2_0", [P, SLOTS, HALF], F32)]
        z2_grouped = [sb("z2_grouped%d" % h, [P, HALF * SLOTS], BF16) for h in range(2)]
        z2s = [sb("z2s%d" % h, [P, HALF], U8) for h in range(2)]

        def z2_half(h):
            for t in range(SLOTS):
                plain = ym[t ^ 1][:, S + h * HALF : S + (h + 1) * HALF]
                nc.vector.tensor_tensor(z2[h][:, t, :], ym[t][:].indirect(half_list(n3_t, h)), plain, ADD)

        a_ps = [psum.tile([P, S], F32, name="ab%d" % t) for t in range(SLOTS)]
        b_ps = [psum.tile([P, S], F32, name="yb%d" % t) for t in range(SLOTS)]
        a_sb = [sb("a_sb%d" % t, [P, S], F32) for t in range(SLOTS)]
        b_sb = [sb("b_sb%d" % t, [P, S], F32) for t in range(SLOTS)]

        z2_half(0)
        interleave(nc, z2_grouped[0][:], z2[0][:])
        w23s = sb("w23s", [P, N], U8, tag="z_term%d" % LAST)
        deal(nc, w23s[:], w23s_raw[:], LINE_BYTES)
        nc.vector.quantize_mx(out=zw[:].bitcast(FP8X4), scales=zs[:], in_=z_grouped[:])
        for t in range(SLOTS):
            product(nc, a_ps[t][:], w2w[:, slot_cols(t)], w23s[W2_FIRST:P, slot_cols(t)], zw[:], zs[:])
            if t < LAST:
                nc.scalar.activation(out=a_sb[t][:], in_=a_ps[t][:], func=COPY)
        z2.append(sb("z2_1", [P, SLOTS, HALF], F32, tag="z_grouped"))
        z2_half(1)
        interleave(nc, z2_grouped[1][:], z2[1][:])

        z2w = [sb("z2w0", [P, HALF], U32, tag="ym%d" % (LAST ^ 1)), sb("z2w1", [P, HALF], U32)]

        def b_half(h):
            nc.vector.quantize_mx(out=z2w[h][:].bitcast(FP8X4), scales=z2s[h][:], in_=z2_grouped[h][:])
            for t in range(SLOTS):
                product(nc, b_ps[t][:, half_cols(h)], w3w[:, slot_cols(t)], w23s[W3_FIRST:P, slot_cols(t)], z2w[h][:], z2s[h][:])

        def a_gather(t):
            nc.vector.tensor_scalar(a_term[t][:], a_sb[t][:].indirect(n4_t[:]), -0.5, 0.0, MULT, ADD)

        b_half(0)
        a_term = [sb("a_term%d" % t, [P, W], F32) for t in range(2)]
        b_term = [sb("b_term%d" % t, [P, W], F32) for t in range(SLOTS)]
        a_gather(0)
        a_gather(1)
        nc.scalar.activation(out=b_sb[0][:, :HALF], in_=b_ps[0][:, :HALF], func=COPY)
        nc.scalar.activation(out=a_sb[LAST][:], in_=a_ps[LAST][:], func=COPY)
        b_half(1)
        a_term.append(sb("a_term2", [P, W], F32, tag="z2_grouped1"))
        a_term.append(sb("a_term3", [P, W], F32))
        a_gather(2)
        a_gather(3)
        nc.scalar.activation(out=b_sb[0][:, HALF:], in_=b_ps[0][:, HALF:], func=COPY)
        for t in range(1, SLOTS):
            nc.scalar.activation(out=b_sb[t][:], in_=b_ps[t][:], func=COPY)

        out_grouped = [sb("out_grouped%d" % h, [P, HALF, SLOTS], BF16) for h in range(2)]
        out_words = sb("out_words", [P, S], I32)
        out_scales = sb("out_scales", [P, S], U8)
        out_slots = out_0.rearrange("(p t) c -> p t c", t=SLOTS)

        nc.vector.tensor_copy(b_term[0][:], b_sb[0][:].indirect(n5_t[:]))
        for t in range(SLOTS):
            if t < LAST:
                nc.vector.tensor_copy(b_term[t + 1][:], b_sb[t + 1][:].indirect(n5_t[:]))
            nc.vector.tensor_tensor(a_sb[t][:].indirect(n4_t[:]), b_term[t][:], a_term[t][:], ADD)
            nc.sync.dma_start(out=out_slots[:, t, :], in_=a_sb[t][:])
            if t // 2 == LAST // 2:
                nc.vector.tensor_copy(out=out_grouped[0][:, :, t], in_=a_sb[t][:, :HALF])
            else:
                nc.scalar.activation(out=out_grouped[0][:, :, t], in_=a_sb[t][:, :HALF], func=COPY)
            nc.scalar.activation(out=out_grouped[1][:, :, t], in_=a_sb[t][:, HALF:], func=COPY)

        for h in range(2):
            grouped = out_grouped[h][:].rearrange("p c t -> p (c t)")
            nc.vector.quantize_mx(out=out_words[:, half_cols(h)].bitcast(FP8X4), scales=out_scales[:, half_cols(h)], in_=grouped)
            nc.sync.dma_start(out=word_view(out_1)[:, half_cols(h)], in_=out_words[:, half_cols(h)])
        for r in range(4):
            queue = nc.scalar if r % 2 else nc.sync
            queue.dma_start(out=out_2[0, r::4, :].bitcast(I32), in_=out_scales[r:P:QUADRANT, :].bitcast(I32))
